import numpy as np
import ml_dtypes


def mxq(x, axis, fmt="e4m3"):
    dtype, down = {"e4m3": (ml_dtypes.float8_e4m3fn, 7), "e5m2": (ml_dtypes.float8_e5m2, 14)}[fmt]
    v = np.moveaxis(np.asarray(x, np.float32).astype(ml_dtypes.bfloat16).astype(np.float64), axis, -1)
    blocks = v.reshape(v.shape[:-1] + (-1, 32))
    amax = np.abs(blocks).max(-1, keepdims=True)
    byte = np.maximum(np.where(amax > 0, np.frexp(amax)[1] - 1 + 127, 0) - down, 1)
    scale = np.exp2(byte - 127.0)
    codes = (blocks / scale).astype(np.float32).astype(dtype).astype(np.float64)
    return np.moveaxis((codes * scale).reshape(v.shape), -1, axis)


WIDE = False


def mx_kscale(k):
    if not WIDE:
        return np.ones(k)
    levels = np.array([10, -10, 5, -5, 0])
    if k % 512:
        return np.exp2(np.random.permutation(np.resize(levels, k // 32))).repeat(32)
    a = np.empty((k // 512, 16))
    for p in range(k // 512):
        a[p, :8] = np.random.permutation(np.resize(levels, 8))
        for g in range(8):
            far = levels[np.abs(levels - a[p, g]) >= 10]
            a[p, g + 8] = far[np.random.randint(len(far))]
    return np.exp2(a.ravel()).repeat(32)


def f64(x):
    return np.asarray(x).astype(np.float64)


def striped(idx):
    return np.tile(idx.reshape(-1, 16).T, (8, 1)).astype(np.uint16)


def unstriped(offs):
    return offs[:16].T.reshape(-1).astype(np.int64)


def gelu(v):
    return 0.5 * v * (1.0 + np.tanh(np.sqrt(2.0 / np.pi) * (v + 0.044715 * v**3)))


K, T, E, C, N = 512, 512, 4, 256, 512


def by_expert(wq, xq):
    return np.concatenate([wq[e].T @ xq[:, e * C:(e + 1) * C] for e in range(E)], axis=1)


def setup_inputs():
    n = np.random.standard_normal
    s = mx_kscale(K)[:, None]
    first = np.random.permutation(np.repeat(np.arange(E), T // E))
    second = (first + 1 + np.random.permutation(np.repeat(np.arange(E - 1), -(-T // (E - 1)))[:T])) % E
    while np.bincount(second, minlength=E).max() != T // E:
        load = np.bincount(second, minlength=E); hi, lo = int(load.argmax()), int(load.argmin())
        t = np.flatnonzero((second == hi) & (first != lo))[0]; second[t] = lo
    slot_token = np.empty(E * C, np.int64); pos = np.empty((2, T), np.int64); fill = np.zeros(E, np.int64)
    place = np.stack([np.random.permutation(C) for _ in range(E)])
    for r, deal in enumerate((first, second)):
        for t in np.random.permutation(T):
            e = deal[t]; j = e * C + place[e, fill[e]]; fill[e] += 1; slot_token[j] = t; pos[r, t] = j
    g = np.random.uniform(0.2, 0.8, T)
    return {
        "xT": (n((K, T)) * s).astype(np.float32),
        "w": (n((E, K, N)) / np.sqrt(K) / s[None]).astype(np.float32),
        "b": (0.3 * n((N, E))).astype(np.float32),
        "gate": np.stack([np.tile(g, (N, 1)), np.tile(1.0 - g, (N, 1))]).astype(np.float32),
        "offs": striped(slot_token),
        "pos1": striped(pos[0]),
        "pos2": striped(pos[1]),
    }


def reference(xT, w, b, gate, offs, pos1, pos2):
    idx = unstriped(offs)
    xq = mxq(f64(xT)[:, idx], 0, "e4m3")
    y = by_expert(mxq(f64(w), 1, "e4m3"), xq)
    y = gelu(y + np.repeat(f64(b), C, axis=1))
    return f64(gate[0]) * y[:, unstriped(pos1)] + f64(gate[1]) * y[:, unstriped(pos2)]

@@ -1,0 +1,160 @@
+from contextlib import ExitStack
+
+import concourse.mybir as mybir
+
+K, T, E, C, N = 512, 512, 4, 256, 512
+P = 128
+PACK = 4
+SLOTS = E * C
+BLOCKS = N // P
+HALF = N // 2
+
+FLOPS = 2 * K * N * SLOTS
+
+F32 = mybir.dt.float32
+BF16 = mybir.dt.bfloat16
+U32 = mybir.dt.uint32
+U16 = mybir.dt.uint16
+U8 = mybir.dt.uint8
+FP8X4 = mybir.dt.float8_e4m3fn_x4
+GELU = mybir.ActivationFunctionType.Gelu_apprx_tanh
+MULT = mybir.AluOpType.mult
+ADD = mybir.AluOpType.add
+
+CUTS = (0, 384, 768, 1024)
+CAST = {(0, 0): "S", (0, 1): "S", (0, 2): "S", (0, 3): "S", (1, 0): "S", (1, 1): "S", (1, 2): "V", (1, 3): "S"}
+
+
+def interleave(nc, engine, grouped, raw):
+    dst = grouped.rearrange("p (c i) t -> p c t i", i=4)
+    src = raw.rearrange("p t (c i) -> p c t i", i=4)
+    if engine == "S":
+        nc.scalar.copy(out=dst, in_=src)
+    elif engine == "V":
+        nc.vector.tensor_copy(out=dst, in_=src)
+    else:
+        nc.gpsimd.tensor_scalar(out=dst, in0=src, scalar1=1.0, scalar2=0.0, op0=MULT, op1=ADD)
+
+
+def tile_routed_moe_kernel(tc, xT, w, b, gate, offs, pos1, pos2, out):
+    nc = tc.nc
+    with ExitStack() as ctx:
+        keep = ctx.enter_context(tc.tile_pool(name="keep", bufs=1))
+        psum = ctx.enter_context(tc.psum_pool(name="psum", bufs=1))
+
+        offs_sb = keep.tile([P, SLOTS // 16], U16, name="offs_sb")
+        pos1_sb = keep.tile([P, T // 16], U16, name="pos1_sb")
+        pos2_sb = keep.tile([P, T // 16], U16, name="pos2_sb")
+        b_sb = keep.tile([P, BLOCKS, E], F32, name="b_sb")
+
+        warm = keep.tile([P, 1], F32, name="warm")
+        warm_out = keep.tile([P, 1], F32, name="warm_out")
+        nc.vector.memset(warm[:], 0.0)
+        nc.scalar.activation(warm_out[:], warm[:], GELU)
+
+        x_words = keep.tile([P, T], U32, name="x_words", align_bytes=64)
+        x_bytes = keep.tile([P, T], U8, name="x_bytes", align_bytes=64)
+        nc.gpsimd.memset(x_bytes[:], 0)
+
+        x_view = xT.rearrange("(p t) n -> p t n", t=PACK)
+        x_raw = []
+        for c in range(2):
+            raw = keep.tile([P, PACK, T // 2], F32, name="x_raw%d" % c)
+            nc.sync.dma_start(raw[:], x_view[:, :, c * (T // 2):(c + 1) * (T // 2)])
+            x_raw.append(raw)
+        nc.sync.dma_start(offs_sb[:], offs)
+
+        w_raw = {}
+        gates = {}
+        gate_view = gate.rearrange("g (q p) t -> q p g t", p=P)
+
+        def load_w(h):
+            for e in range(E):
+                raw = keep.tile([P, PACK, HALF], F32, name="w_raw%d_%d" % (h, e))
+                nc.sync.dma_start(raw[:], w[e].rearrange("(p t) n -> p t n", t=PACK)[:, :, h * HALF:(h + 1) * HALF])
+                w_raw[h, e] = raw
+
+        def load_gate(q):
+            g = keep.tile([P, 2, T], F32, name="gate%d" % q)
+            nc.sync.dma_start(g[:], gate_view[q])
+            gates[q] = g
+
+        load_w(0)
+        nc.sync.dma_start(b_sb[:], b.rearrange("(q p) e -> p q e", p=P))
+        nc.sync.dma_start(pos1_sb[:], pos1)
+        nc.sync.dma_start(pos2_sb[:], pos2)
+        load_gate(0)
+        load_w(1)
+        load_gate(1)
+        load_gate(2)
+        load_gate(3)
+
+        H = T // 2
+        grouped = []
+        for c in range(2):
+            g = keep.tile([P, H, PACK], BF16, name="x_grouped%d" % c, align_bytes=64)
+            grouped.append(g)
+        interleave(nc, "V", grouped[0][:], x_raw[0][:])
+        interleave(nc, "V", grouped[1][:, 0:H // 2, :], x_raw[1][:, :, 0:H // 2])
+        interleave(nc, "S", grouped[1][:, H // 2:H, :], x_raw[1][:, :, H // 2:H])
+        for c in range(2):
+            nc.vector.quantize_mx(
+                out=x_words[:, c * H:(c + 1) * H].bitcast(FP8X4),
+                scales=x_bytes[:, c * H:(c + 1) * H],
+                in_=grouped[c][:].rearrange("p n t -> p (n t)"),
+            )
+        s_words = keep.tile([P, SLOTS], U32, name="s_words", align_bytes=64)
+        s_bytes = keep.tile([P, SLOTS], U8, name="s_bytes", align_bytes=64)
+        for lo, hi in zip(CUTS[:-1], CUTS[1:]):
+            part = offs_sb[:, lo // 16:hi // 16]
+            nc.vector.tensor_copy(s_words[:, lo:hi], x_words[:].indirect(part))
+            nc.vector.tensor_copy(s_bytes[:, lo:hi], x_bytes[:].indirect(part))
+
+        for h in range(2):
+            codes = {}
+            for e in range(E):
+                wg = keep.tile([P, HALF, PACK], BF16, name="w_grouped%d_%d" % (h, e), align_bytes=64)
+                interleave(nc, CAST[h, e], wg[:], w_raw[h, e][:])
+                w_words = keep.tile([P, HALF], U32, name="w_words%d_%d" % (h, e), align_bytes=64)
+                w_bytes = keep.tile([P, HALF], U8, name="w_bytes%d_%d" % (h, e), align_bytes=64)
+                nc.vector.quantize_mx(
+                    out=w_words[:].bitcast(FP8X4), scales=w_bytes[:], in_=wg[:].rearrange("p n t -> p (n t)"))
+                codes[e] = (w_words, w_bytes)
+            banks = {}
+            for q in (2 * h, 2 * h + 1):
+                for d in range(2):
+                    bank = psum.tile([P, 2 * C], F32, name="bank%d_%d" % (q, d))
+                    banks[q, d] = bank
+            ys = {}
+            for q in (2 * h, 2 * h + 1):
+                y = keep.tile([P, SLOTS], F32, name="y%d" % q)
+                ys[q] = y
+                cols = slice((q - 2 * h) * P, (q - 2 * h + 1) * P)
+                for e in range(E):
+                    slots = slice(e * C, (e + 1) * C)
+                    acc = banks[q, e // 2][:, (e % 2) * C:(e % 2 + 1) * C]
+                    w_words, w_bytes = codes[e]
+                    nc.tensor.matmul_mx(
+                        out=acc,
+                        lhsT=w_words[:, cols].bitcast(FP8X4),
+                        lhsT_scale=w_bytes[:, cols],
+                        rhs=s_words[:, slots].bitcast(FP8X4),
+                        rhs_scale=s_bytes[:, slots],
+                        start=True,
+                        stop=True,
+                    )
+                    nc.scalar.activation(y[:, slots], acc, GELU, bias=b_sb[:, q, e:e + 1])
+            for q in (2 * h, 2 * h + 1):
+                r = keep.tile([P, T], F32, name="r%d" % q)
+                g1 = keep.tile([P, T], F32, name="g1_%d" % q)
+                g2 = keep.tile([P, T], F32, name="g2_%d" % q)
+                nc.vector.tensor_tensor(g1[:], ys[q][:].indirect(pos1_sb[:]), gates[q][:, 0, :], MULT)
+                if q < BLOCKS - 1:
+                    pieces = ((0, T),)
+                else:
+                    pieces = ((0, T // 2), (T // 2, T))
+                for lo, hi in pieces:
+                    nc.vector.tensor_tensor(
+                        g2[:, lo:hi], ys[q][:].indirect(pos2_sb[:, lo // 16:hi // 16]), gates[q][:, 1, lo:hi], MULT)
+                    nc.vector.tensor_tensor(r[:, lo:hi], g1[:, lo:hi], g2[:, lo:hi], ADD)
+                    nc.sync.dma_start(out[q * P:(q + 1) * P, lo:hi], r[:, lo:hi])

@@ -21,26 +21,31 @@ GELU = mybir.ActivationFunctionType.Gelu_apprx_tanh
 MULT = mybir.AluOpType.mult
 ADD = mybir.AluOpType.add
 
-CUTS = (0, 384, 768, 1024)
-CAST = {(0, 0): "S", (0, 1): "S", (0, 2): "S", (0, 3): "S", (1, 0): "S", (1, 1): "S", (1, 2): "V", (1, 3): "S"}
+CAST = {(0, 0): "S", (0, 1): "S", (0, 2): "S", (0, 3): "S", (1, 0): "V", (1, 1): "S", (1, 2): "S", (1, 3): "S"}
+XCHUNKS = ((0, 256), (256, 384), (384, 512))
+XCAST = ("V", "S", "V")
+AT = {"raw02":0,"raw03":4096,"y0":2048,"y1":6144,"raw12":10240,"raw13":14336,"y2":12288,"y3":16384,"w_grouped02":20480,"s_words3":20480,"s_bytes3":21504,"w_grouped03":22528,"w_grouped10":22528,"w_grouped12":24576,"w_grouped13":26624,"g2_1":25600}
 
 
 def interleave(nc, engine, grouped, raw):
-    dst = grouped.rearrange("p (c i) t -> p c t i", i=4)
-    src = raw.rearrange("p t (c i) -> p c t i", i=4)
-    if engine == "S":
-        nc.scalar.copy(out=dst, in_=src)
-    elif engine == "V":
-        nc.vector.tensor_copy(out=dst, in_=src)
-    else:
-        nc.gpsimd.tensor_scalar(out=dst, in0=src, scalar1=1.0, scalar2=0.0, op0=MULT, op1=ADD)
+    if engine == "G":
+        nc.gpsimd.tensor_scalar(out=grouped, in0=raw.rearrange("p t c -> p c t"), scalar1=1.0, scalar2=0.0, op0=MULT, op1=ADD)
+        return
+    copy = nc.scalar.copy if engine == "S" else nc.vector.tensor_copy
+    copy(out=grouped.rearrange("p (c i) t -> p c t i", i=4), in_=raw.rearrange("p t (c i) -> p c t i", i=4))
 
 
 def tile_routed_moe_kernel(tc, xT, w, b, gate, offs, pos1, pos2, out):
     nc = tc.nc
     with ExitStack() as ctx:
         keep = ctx.enter_context(tc.tile_pool(name="keep", bufs=1))
+        lay = ctx.enter_context(tc.tile_pool(name="lay", bufs=1))
         psum = ctx.enter_context(tc.psum_pool(name="psum", bufs=1))
+
+        def held(shape, dtype, name):
+            if name in AT:
+                return lay.tile(shape, dtype, name=name, align_bytes=64, offset=AT[name])
+            return keep.tile(shape, dtype, name=name, align_bytes=64)
 
         offs_sb = keep.tile([P, SLOTS // 16], U16, name="offs_sb")
         pos1_sb = keep.tile([P, T // 16], U16, name="pos1_sb")
@@ -52,15 +57,15 @@ def tile_routed_moe_kernel(tc, xT, w, b, gate, offs, pos1, pos2, out):
         nc.vector.memset(warm[:], 0.0)
         nc.scalar.activation(warm_out[:], warm[:], GELU)
 
-        x_words = keep.tile([P, T], U32, name="x_words", align_bytes=64)
-        x_bytes = keep.tile([P, T], U8, name="x_bytes", align_bytes=64)
+        x_words = held([P, T], U32, "x_words")
+        x_bytes = held([P, T], U8, "x_bytes")
         nc.gpsimd.memset(x_bytes[:], 0)
 
         x_view = xT.rearrange("(p t) n -> p t n", t=PACK)
         x_raw = []
-        for c in range(2):
-            raw = keep.tile([P, PACK, T // 2], F32, name="x_raw%d" % c)
-            nc.sync.dma_start(raw[:], x_view[:, :, c * (T // 2):(c + 1) * (T // 2)])
+        for lo, hi in XCHUNKS:
+            raw = held([P, PACK, hi - lo], F32, "x_raw%d" % lo)
+            nc.sync.dma_start(raw[:], x_view[:, :, lo:hi])
             x_raw.append(raw)
         nc.sync.dma_start(offs_sb[:], offs)
 
@@ -68,93 +73,132 @@ def tile_routed_moe_kernel(tc, xT, w, b, gate, offs, pos1, pos2, out):
         gates = {}
         gate_view = gate.rearrange("g (q p) t -> q p g t", p=P)
 
-        def load_w(h):
-            for e in range(E):
-                raw = keep.tile([P, PACK, HALF], F32, name="w_raw%d_%d" % (h, e))
-                nc.sync.dma_start(raw[:], w[e].rearrange("(p t) n -> p t n", t=PACK)[:, :, h * HALF:(h + 1) * HALF])
-                w_raw[h, e] = raw
+        def load_w(h, e):
+            raw = held([P, PACK, HALF], F32, "raw%d%d" % (h, e))
+            nc.sync.dma_start(raw[:], w[e].rearrange("(p t) n -> p t n", t=PACK)[:, :, h * HALF:(h + 1) * HALF])
+            w_raw[h, e] = raw
 
         def load_gate(q):
-            g = keep.tile([P, 2, T], F32, name="gate%d" % q)
+            g = held([P, 2, T], F32, "gate%d" % q)
             nc.sync.dma_start(g[:], gate_view[q])
             gates[q] = g
 
-        load_w(0)
+        for e in range(E):
+            load_w(0, e)
+        load_w(1, 0)
         nc.sync.dma_start(b_sb[:], b.rearrange("(q p) e -> p q e", p=P))
         nc.sync.dma_start(pos1_sb[:], pos1)
         nc.sync.dma_start(pos2_sb[:], pos2)
         load_gate(0)
-        load_w(1)
+        load_w(1, 1)
+        load_w(1, 2)
         load_gate(1)
+        load_w(1, 3)
         load_gate(2)
         load_gate(3)
 
-        H = T // 2
         grouped = []
-        for c in range(2):
-            g = keep.tile([P, H, PACK], BF16, name="x_grouped%d" % c, align_bytes=64)
+        for c, (lo, hi) in enumerate(XCHUNKS):
+            g = held([P, hi - lo, PACK], BF16, "x_grouped%d" % c)
             grouped.append(g)
-        interleave(nc, "V", grouped[0][:], x_raw[0][:])
-        interleave(nc, "V", grouped[1][:, 0:H // 2, :], x_raw[1][:, :, 0:H // 2])
-        interleave(nc, "S", grouped[1][:, H // 2:H, :], x_raw[1][:, :, H // 2:H])
-        for c in range(2):
+            interleave(nc, XCAST[c], g[:], x_raw[c][:])
+        for c, (lo, hi) in enumerate(XCHUNKS):
             nc.vector.quantize_mx(
-                out=x_words[:, c * H:(c + 1) * H].bitcast(FP8X4),
-                scales=x_bytes[:, c * H:(c + 1) * H],
+                out=x_words[:, lo:hi].bitcast(FP8X4),
+                scales=x_bytes[:, lo:hi],
                 in_=grouped[c][:].rearrange("p n t -> p (n t)"),
             )
-        s_words = keep.tile([P, SLOTS], U32, name="s_words", align_bytes=64)
-        s_bytes = keep.tile([P, SLOTS], U8, name="s_bytes", align_bytes=64)
-        for lo, hi in zip(CUTS[:-1], CUTS[1:]):
-            part = offs_sb[:, lo // 16:hi // 16]
-            nc.vector.tensor_copy(s_words[:, lo:hi], x_words[:].indirect(part))
-            nc.vector.tensor_copy(s_bytes[:, lo:hi], x_bytes[:].indirect(part))
+        slot_words = {}
+        slot_bytes = {}
 
-        for h in range(2):
-            codes = {}
+        def gather(name, lo, hi, cuts):
+            words = held([P, hi - lo], U32, "s_words" + name)
+            scale = held([P, hi - lo], U8, "s_bytes" + name)
+            for a, z in zip(cuts[:-1], cuts[1:]):
+                part = offs_sb[:, a // 16:z // 16]
+                nc.vector.tensor_copy(words[:, a - lo:z - lo], x_words[:].indirect(part))
+                nc.vector.tensor_copy(scale[:, a - lo:z - lo], x_bytes[:].indirect(part))
+            for e in range(lo // C, hi // C):
+                slot_words[e] = words[:, e * C - lo:(e + 1) * C - lo]
+                slot_bytes[e] = scale[:, e * C - lo:(e + 1) * C - lo]
+
+        ys = {}
+        banks = {}
+        codes = {}
+
+        def weights(h, e):
+            wg = held([P, HALF, PACK], BF16, "w_grouped%d%d" % (h, e))
+            interleave(nc, CAST[h, e], wg[:], w_raw[h, e][:])
+            w_words = held([P, HALF], U32, "w_words%d%d" % (h, e))
+            w_bytes = held([P, HALF], U8, "w_bytes%d%d" % (h, e))
+            nc.vector.quantize_mx(
+                out=w_words[:].bitcast(FP8X4), scales=w_bytes[:], in_=wg[:].rearrange("p n t -> p (n t)"))
+            codes[h, e] = (w_words, w_bytes)
+
+        def expert(q, e):
+            cols = slice((q % 2) * P, (q % 2 + 1) * P)
+            slots = slice(e * C, (e + 1) * C)
+            if e == 0:
+                ys[q] = held([P, SLOTS], F32, "y%d" % q)
+            if e % 2 == 0:
+                banks[q, e // 2] = psum.tile([P, 2 * C], F32, name="bank%d_%d" % (q, e))
+            acc = banks[q, e // 2][:, (e % 2) * C:(e % 2 + 1) * C]
+            w_words, w_bytes = codes[q // 2, e]
+            nc.tensor.matmul_mx(
+                out=acc,
+                lhsT=w_words[:, cols].bitcast(FP8X4),
+                lhsT_scale=w_bytes[:, cols],
+                rhs=slot_words[e].bitcast(FP8X4),
+                rhs_scale=slot_bytes[e],
+                start=True,
+                stop=True,
+            )
+            nc.scalar.activation(ys[q][:, slots], acc, GELU, bias=b_sb[:, q, e:e + 1])
+
+        gather("0", 0, 3 * C, (0, 384, 768))
+        weights(0, 0)
+        weights(0, 1)
+        weights(0, 2)
+        gather("3", 3 * C, SLOTS, (768, 1024))
+        weights(0, 3)
+        for q in (0, 1):
             for e in range(E):
-                wg = keep.tile([P, HALF, PACK], BF16, name="w_grouped%d_%d" % (h, e), align_bytes=64)
-                interleave(nc, CAST[h, e], wg[:], w_raw[h, e][:])
-                w_words = keep.tile([P, HALF], U32, name="w_words%d_%d" % (h, e), align_bytes=64)
-                w_bytes = keep.tile([P, HALF], U8, name="w_bytes%d_%d" % (h, e), align_bytes=64)
-                nc.vector.quantize_mx(
-                    out=w_words[:].bitcast(FP8X4), scales=w_bytes[:], in_=wg[:].rearrange("p n t -> p (n t)"))
-                codes[e] = (w_words, w_bytes)
-            banks = {}
-            for q in (2 * h, 2 * h + 1):
-                for d in range(2):
-                    bank = psum.tile([P, 2 * C], F32, name="bank%d_%d" % (q, d))
-                    banks[q, d] = bank
-            ys = {}
-            for q in (2 * h, 2 * h + 1):
-                y = keep.tile([P, SLOTS], F32, name="y%d" % q)
-                ys[q] = y
-                cols = slice((q - 2 * h) * P, (q - 2 * h + 1) * P)
-                for e in range(E):
-                    slots = slice(e * C, (e + 1) * C)
-                    acc = banks[q, e // 2][:, (e % 2) * C:(e % 2 + 1) * C]
-                    w_words, w_bytes = codes[e]
-                    nc.tensor.matmul_mx(
-                        out=acc,
-                        lhsT=w_words[:, cols].bitcast(FP8X4),
-                        lhsT_scale=w_bytes[:, cols],
-                        rhs=s_words[:, slots].bitcast(FP8X4),
-                        rhs_scale=s_bytes[:, slots],
-                        start=True,
-                        stop=True,
-                    )
-                    nc.scalar.activation(y[:, slots], acc, GELU, bias=b_sb[:, q, e:e + 1])
-            for q in (2 * h, 2 * h + 1):
-                r = keep.tile([P, T], F32, name="r%d" % q)
-                g1 = keep.tile([P, T], F32, name="g1_%d" % q)
-                g2 = keep.tile([P, T], F32, name="g2_%d" % q)
-                nc.vector.tensor_tensor(g1[:], ys[q][:].indirect(pos1_sb[:]), gates[q][:, 0, :], MULT)
-                if q < BLOCKS - 1:
-                    pieces = ((0, T),)
-                else:
-                    pieces = ((0, T // 2), (T // 2, T))
-                for lo, hi in pieces:
-                    nc.vector.tensor_tensor(
-                        g2[:, lo:hi], ys[q][:].indirect(pos2_sb[:, lo // 16:hi // 16]), gates[q][:, 1, lo:hi], MULT)
-                    nc.vector.tensor_tensor(r[:, lo:hi], g1[:, lo:hi], g2[:, lo:hi], ADD)
-                    nc.sync.dma_start(out[q * P:(q + 1) * P, lo:hi], r[:, lo:hi])
+                expert(q, e)
+        for e in range(E):
+            weights(1, e)
+        for q in (2, 3):
+            for e in range(E):
+                expert(q, e)
+
+        firsts = {}
+        seconds = {}
+
+        def first(q):
+            g1 = held([P, T], F32, "g1_%d" % q)
+            nc.vector.tensor_tensor(g1[:], ys[q][:].indirect(pos1_sb[:]), gates[q][:, 0, :], MULT)
+            firsts[q] = g1
+
+        def second(q, lo, hi):
+            if q not in seconds:
+                seconds[q] = held([P, T], F32, "g2_%d" % q)
+            nc.vector.tensor_tensor(
+                seconds[q][:, lo:hi], ys[q][:].indirect(pos2_sb[:, lo // 16:hi // 16]), gates[q][:, 1, lo:hi], MULT)
+
+        def add(q, lo, hi):
+            r = held([P, hi - lo], F32, "r%d_%d" % (q, lo))
+            nc.vector.tensor_tensor(r[:], firsts[q][:, lo:hi], seconds[q][:, lo:hi], ADD)
+            nc.sync.dma_start(out[q * P:(q + 1) * P, lo:hi], r[:])
+
+        first(0)
+        second(0, 0, T)
+        for q in range(1, BLOCKS):
+            first(q)
+            add(q - 1, 0, T)
+            if q < BLOCKS - 1:
+                second(q, 0, T)
+        last = BLOCKS - 1
+        pieces = ((0, T // 2), (T // 2, T))
+        for lo, hi in pieces:
+            second(last, lo, hi)
+        for lo, hi in pieces:
+            add(last, lo, hi)

@@ -85,8 +85,8 @@ def tile_routed_moe_kernel(tc, xT, w, b, gate, offs, pos1, pos2, out):
 
         for e in range(E):
             load_w(0, e)
-        load_w(1, 0)
         nc.sync.dma_start(b_sb[:], b.rearrange("(q p) e -> p q e", p=P))
+        load_w(1, 0)
         nc.sync.dma_start(pos1_sb[:], pos1)
         nc.sync.dma_start(pos2_sb[:], pos2)
         load_gate(0)
@@ -135,17 +135,13 @@ def tile_routed_moe_kernel(tc, xT, w, b, gate, offs, pos1, pos2, out):
                 out=w_words[:].bitcast(FP8X4), scales=w_bytes[:], in_=wg[:].rearrange("p n t -> p (n t)"))
             codes[h, e] = (w_words, w_bytes)
 
-        def expert(q, e):
+        def multiply(q, e):
+            if (q // 2, e) not in banks:
+                banks[q // 2, e] = psum.tile([P, 2, C], F32, name="bank%d_%d" % (q // 2, e))
             cols = slice((q % 2) * P, (q % 2 + 1) * P)
-            slots = slice(e * C, (e + 1) * C)
-            if e == 0:
-                ys[q] = held([P, SLOTS], F32, "y%d" % q)
-            if e % 2 == 0:
-                banks[q, e // 2] = psum.tile([P, 2 * C], F32, name="bank%d_%d" % (q, e))
-            acc = banks[q, e // 2][:, (e % 2) * C:(e % 2 + 1) * C]
             w_words, w_bytes = codes[q // 2, e]
             nc.tensor.matmul_mx(
-                out=acc,
+                out=banks[q // 2, e][:, q % 2, :],
                 lhsT=w_words[:, cols].bitcast(FP8X4),
                 lhsT_scale=w_bytes[:, cols],
                 rhs=slot_words[e].bitcast(FP8X4),
@@ -153,7 +149,24 @@ def tile_routed_moe_kernel(tc, xT, w, b, gate, offs, pos1, pos2, out):
                 start=True,
                 stop=True,
             )
-            nc.scalar.activation(ys[q][:, slots], acc, GELU, bias=b_sb[:, q, e:e + 1])
+
+        def activate(q, e):
+            if q not in ys:
+                ys[q] = held([P, SLOTS], F32, "y%d" % q)
+            nc.scalar.activation(
+                ys[q][:, e * C:(e + 1) * C], banks[q // 2, e][:, q % 2, :], GELU, bias=b_sb[:, q, e:e + 1])
+
+        def half(h):
+            first_q, second_q = 2 * h, 2 * h + 1
+            for e in range(E - 1):
+                multiply(first_q, e)
+                multiply(second_q, e)
+            multiply(first_q, E - 1)
+            for e in range(E):
+                activate(first_q, e)
+            multiply(second_q, E - 1)
+            for e in range(E):
+                activate(second_q, e)
 
         gather("0", 0, 3 * C, (0, 384, 768))
         weights(0, 0)
@@ -161,14 +174,10 @@ def tile_routed_moe_kernel(tc, xT, w, b, gate, offs, pos1, pos2, out):
         weights(0, 2)
         gather("3", 3 * C, SLOTS, (768, 1024))
         weights(0, 3)
-        for q in (0, 1):
-            for e in range(E):
-                expert(q, e)
+        half(0)
         for e in range(E):
             weights(1, e)
-        for q in (2, 3):
-            for e in range(E):
-                expert(q, e)
+        half(1)
 
         firsts = {}
         seconds = {}

from contextlib import ExitStack

import concourse.mybir as mybir

K, T, E, C, N = 512, 512, 4, 256, 512
P = 128
PACK = 4
SLOTS = E * C
BLOCKS = N // P
HALF = N // 2

FLOPS = 2 * K * N * SLOTS

F32 = mybir.dt.float32
BF16 = mybir.dt.bfloat16
U32 = mybir.dt.uint32
U16 = mybir.dt.uint16
U8 = mybir.dt.uint8
FP8X4 = mybir.dt.float8_e4m3fn_x4
GELU = mybir.ActivationFunctionType.Gelu_apprx_tanh
MULT = mybir.AluOpType.mult
ADD = mybir.AluOpType.add

CAST = {(0, 0): "S", (0, 1): "S", (0, 2): "S", (0, 3): "S", (1, 0): "V", (1, 1): "S", (1, 2): "S", (1, 3): "S"}
XCHUNKS = ((0, 256), (256, 384), (384, 512))
XCAST = ("V", "S", "V")
AT = {"raw02":0,"raw03":4096,"y0":2048,"y1":6144,"raw12":10240,"raw13":14336,"y2":12288,"y3":16384,"w_grouped02":20480,"s_words3":20480,"s_bytes3":21504,"w_grouped03":22528,"w_grouped10":22528,"w_grouped12":24576,"w_grouped13":26624,"g2_1":25600}


def interleave(nc, engine, grouped, raw):
    if engine == "G":
        nc.gpsimd.tensor_scalar(out=grouped, in0=raw.rearrange("p t c -> p c t"), scalar1=1.0, scalar2=0.0, op0=MULT, op1=ADD)
        return
    copy = nc.scalar.copy if engine == "S" else nc.vector.tensor_copy
    copy(out=grouped.rearrange("p (c i) t -> p c t i", i=4), in_=raw.rearrange("p t (c i) -> p c t i", i=4))


def tile_routed_moe_kernel(tc, xT, w, b, gate, offs, pos1, pos2, out):
    nc = tc.nc
    with ExitStack() as ctx:
        keep = ctx.enter_context(tc.tile_pool(name="keep", bufs=1))
        lay = ctx.enter_context(tc.tile_pool(name="lay", bufs=1))
        psum = ctx.enter_context(tc.psum_pool(name="psum", bufs=1))

        def held(shape, dtype, name):
            if name in AT:
                return lay.tile(shape, dtype, name=name, align_bytes=64, offset=AT[name])
            return keep.tile(shape, dtype, name=name, align_bytes=64)

        offs_sb = keep.tile([P, SLOTS // 16], U16, name="offs_sb")
        pos1_sb = keep.tile([P, T // 16], U16, name="pos1_sb")
        pos2_sb = keep.tile([P, T // 16], U16, name="pos2_sb")
        b_sb = keep.tile([P, BLOCKS, E], F32, name="b_sb")

        warm = keep.tile([P, 1], F32, name="warm")
        warm_out = keep.tile([P, 1], F32, name="warm_out")
        nc.vector.memset(warm[:], 0.0)
        nc.scalar.activation(warm_out[:], warm[:], GELU)

        x_words = held([P, T], U32, "x_words")
        x_bytes = held([P, T], U8, "x_bytes")
        nc.gpsimd.memset(x_bytes[:], 0)

        x_view = xT.rearrange("(p t) n -> p t n", t=PACK)
        x_raw = []
        for lo, hi in XCHUNKS:
            raw = held([P, PACK, hi - lo], F32, "x_raw%d" % lo)
            nc.sync.dma_start(raw[:], x_view[:, :, lo:hi])
            x_raw.append(raw)
        nc.sync.dma_start(offs_sb[:], offs)

        w_raw = {}
        gates = {}
        gate_view = gate.rearrange("g (q p) t -> q p g t", p=P)

        def load_w(h, e):
            raw = held([P, PACK, HALF], F32, "raw%d%d" % (h, e))
            nc.sync.dma_start(raw[:], w[e].rearrange("(p t) n -> p t n", t=PACK)[:, :, h * HALF:(h + 1) * HALF])
            w_raw[h, e] = raw

        def load_gate(q):
            g = held([P, 2, T], F32, "gate%d" % q)
            nc.sync.dma_start(g[:], gate_view[q])
            gates[q] = g

        for e in range(E):
            load_w(0, e)
        nc.sync.dma_start(b_sb[:], b.rearrange("(q p) e -> p q e", p=P))
        load_w(1, 0)
        nc.sync.dma_start(pos1_sb[:], pos1)
        nc.sync.dma_start(pos2_sb[:], pos2)
        load_gate(0)
        load_w(1, 1)
        load_w(1, 2)
        load_gate(1)
        load_w(1, 3)
        load_gate(2)
        load_gate(3)

        grouped = []
        for c, (lo, hi) in enumerate(XCHUNKS):
            g = held([P, hi - lo, PACK], BF16, "x_grouped%d" % c)
            grouped.append(g)
            interleave(nc, XCAST[c], g[:], x_raw[c][:])
        for c, (lo, hi) in enumerate(XCHUNKS):
            nc.vector.quantize_mx(
                out=x_words[:, lo:hi].bitcast(FP8X4),
                scales=x_bytes[:, lo:hi],
                in_=grouped[c][:].rearrange("p n t -> p (n t)"),
            )
        slot_words = {}
        slot_bytes = {}

        def gather(name, lo, hi, cuts):
            words = held([P, hi - lo], U32, "s_words" + name)
            scale = held([P, hi - lo], U8, "s_bytes" + name)
            for a, z in zip(cuts[:-1], cuts[1:]):
                part = offs_sb[:, a // 16:z // 16]
                nc.vector.tensor_copy(words[:, a - lo:z - lo], x_words[:].indirect(part))
                nc.vector.tensor_copy(scale[:, a - lo:z - lo], x_bytes[:].indirect(part))
            for e in range(lo // C, hi // C):
                slot_words[e] = words[:, e * C - lo:(e + 1) * C - lo]
                slot_bytes[e] = scale[:, e * C - lo:(e + 1) * C - lo]

        ys = {}
        banks = {}
        codes = {}

        def weights(h, e):
            wg = held([P, HALF, PACK], BF16, "w_grouped%d%d" % (h, e))
            interleave(nc, CAST[h, e], wg[:], w_raw[h, e][:])
            w_words = held([P, HALF], U32, "w_words%d%d" % (h, e))
            w_bytes = held([P, HALF], U8, "w_bytes%d%d" % (h, e))
            nc.vector.quantize_mx(
                out=w_words[:].bitcast(FP8X4), scales=w_bytes[:], in_=wg[:].rearrange("p n t -> p (n t)"))
            codes[h, e] = (w_words, w_bytes)

        def multiply(q, e):
            if (q // 2, e) not in banks:
                banks[q // 2, e] = psum.tile([P, 2, C], F32, name="bank%d_%d" % (q // 2, e))
            cols = slice((q % 2) * P, (q % 2 + 1) * P)
            w_words, w_bytes = codes[q // 2, e]
            nc.tensor.matmul_mx(
                out=banks[q // 2, e][:, q % 2, :],
                lhsT=w_words[:, cols].bitcast(FP8X4),
                lhsT_scale=w_bytes[:, cols],
                rhs=slot_words[e].bitcast(FP8X4),
                rhs_scale=slot_bytes[e],
                start=True,
                stop=True,
            )

        def activate(q, e):
            if q not in ys:
                ys[q] = held([P, SLOTS], F32, "y%d" % q)
            nc.scalar.activation(
                ys[q][:, e * C:(e + 1) * C], banks[q // 2, e][:, q % 2, :], GELU, bias=b_sb[:, q, e:e + 1])

        def half(h):
            first_q, second_q = 2 * h, 2 * h + 1
            for e in range(E - 1):
                multiply(first_q, e)
                multiply(second_q, e)
            multiply(first_q, E - 1)
            for e in range(E):
                activate(first_q, e)
            multiply(second_q, E - 1)
            for e in range(E):
                activate(second_q, e)

        gather("0", 0, 3 * C, (0, 384, 768))
        weights(0, 0)
        weights(0, 1)
        weights(0, 2)
        gather("3", 3 * C, SLOTS, (768, 1024))
        weights(0, 3)
        half(0)
        for e in range(E):
            weights(1, e)
        half(1)

        firsts = {}
        seconds = {}

        def first(q):
            g1 = held([P, T], F32, "g1_%d" % q)
            nc.vector.tensor_tensor(g1[:], ys[q][:].indirect(pos1_sb[:]), gates[q][:, 0, :], MULT)
            firsts[q] = g1

        def second(q, lo, hi):
            if q not in seconds:
                seconds[q] = held([P, T], F32, "g2_%d" % q)
            nc.vector.tensor_tensor(
                seconds[q][:, lo:hi], ys[q][:].indirect(pos2_sb[:, lo // 16:hi // 16]), gates[q][:, 1, lo:hi], MULT)

        def add(q, lo, hi):
            r = held([P, hi - lo], F32, "r%d_%d" % (q, lo))
            nc.vector.tensor_tensor(r[:], firsts[q][:, lo:hi], seconds[q][:, lo:hi], ADD)
            nc.sync.dma_start(out[q * P:(q + 1) * P, lo:hi], r[:])

        first(0)
        second(0, 0, T)
        for q in range(1, BLOCKS):
            first(q)
            add(q - 1, 0, T)
            if q < BLOCKS - 1:
                second(q, 0, T)
        last = BLOCKS - 1
        pieces = ((0, T // 2), (T // 2, T))
        for lo, hi in pieces:
            second(last, lo, hi)
        for lo, hi in pieces:
            add(last, lo, hi)
